import numpy as np
CORES = [1,0]
N = 2
def setup_inputs(rng):
    return {"x": rng.standard_normal((N, 32, 1024), dtype=np.float32)}
def reference(x):
    s = x.sum(axis=0, dtype=np.float64).astype(x.dtype)
    return {"y": np.broadcast_to(s, (N,) + s.shape)}

from concourse.mybir import AluOpType

SCRATCH = {
    "send": ("sbuf", [128, 256], "float32"),
    "land": ("sbuf", [128, 256], "float32"),
}
SEMAPHORES = ["loaded", "copied", "read", "arrived", "stored"]


def rank_program(g, core, T, topo):
    rank = T.rank_of(core)
    if rank is None:
        return
    peer = T.cores[1 - rank]
    rid, pid, sengine = topo.addr(peer)
    mask = topo.mask(core, peer)

    g.dma_start(T.send[:], T.x[:]).then_inc(T.sem.loaded, 16)
    g.dma_start(T.y[:], T.x[:]).then_inc(T.sem.copied, 16)

    g.wait_ge(T.sem.loaded, 16)
    g.remote_dma(T.land[:], T.send[:], T.sem.arrived, T.sem.read, pid, rid, mask)

    g.wait_ge(T.sem.arrived, 16)
    g.wait_ge(T.sem.copied, 16)
    g.dma_start(T.y[:], T.land[:], accum_op=AluOpType.add).then_inc(T.sem.stored, 16)

    g.wait_ge(T.sem.read, 16)
    g.wait_ge(T.sem.stored, 16)
